import numpy as np
import ml_dtypes


def mxq(x, axis, fmt="e4m3"):
    dtype, down = {"e4m3": (ml_dtypes.float8_e4m3fn, 7), "e5m2": (ml_dtypes.float8_e5m2, 14)}[fmt]
    v = np.moveaxis(np.asarray(x, np.float32).astype(ml_dtypes.bfloat16).astype(np.float64), axis, -1)
    blocks = v.reshape(v.shape[:-1] + (-1, 32))
    amax = np.abs(blocks).max(-1, keepdims=True)
    byte = np.maximum(np.where(amax > 0, np.frexp(amax)[1] - 1 + 127, 0) - down, 1)
    scale = np.exp2(byte - 127.0)
    codes = (blocks / scale).astype(np.float32).astype(dtype).astype(np.float64)
    return np.moveaxis((codes * scale).reshape(v.shape), -1, axis)


WIDE = False


def mx_kscale(k):
    if not WIDE:
        return np.ones(k)
    levels = np.array([10, -10, 5, -5, 0])
    if k % 512:
        return np.exp2(np.random.permutation(np.resize(levels, k // 32))).repeat(32)
    a = np.empty((k // 512, 16))
    for p in range(k // 512):
        a[p, :8] = np.random.permutation(np.resize(levels, 8))
        for g in range(8):
            far = levels[np.abs(levels - a[p, g]) >= 10]
            a[p, g + 8] = far[np.random.randint(len(far))]
    return np.exp2(a.ravel()).repeat(32)


def f64(x):
    return np.asarray(x).astype(np.float64)


def striped8(idx):
    return np.concatenate([x.reshape(-1, 16).T for x in idx]).astype(np.uint16)


def runs(offs, k):
    lists = np.stack([offs[16 * r : 16 * r + 16].T.reshape(-1) for r in range(8)]).astype(np.int64)
    return lists[np.arange(k) % 512 // 64]


def pack_weight(w):
    k, n = w.shape
    w = f64(np.asarray(w, np.float32).astype(ml_dtypes.bfloat16)).reshape(k // 32, 32, n)
    amax = np.abs(w).max(1)
    byte = np.clip(np.where(amax > 0, np.frexp(amax)[1] - 1 + 127 - 7, 1), 1, 254)
    scaled = (w * np.exp2(127.0 - byte)[:, None, :]).reshape(k, n).astype(np.float32)
    words = np.ascontiguousarray(scaled.reshape(k // 512, 128, 4, n).transpose(0, 1, 3, 2)).astype(ml_dtypes.float8_e4m3fn).view(np.uint8)
    return words, np.ascontiguousarray(byte.astype(np.uint8).reshape(k // 512, 16, n))


def unpack_weight(words, scales):
    g, p, n, _ = words.shape
    vals = np.ascontiguousarray(words).view(ml_dtypes.float8_e4m3fn).astype(np.float64) * np.repeat(np.exp2(scales.astype(np.float64) - 127.0), 8, axis=1)[..., None]
    return vals.transpose(0, 1, 3, 2).reshape(g * 512, n)


def sigmoid(v):
    return 1.0 / (1.0 + np.exp(-np.maximum(v, -700.0)))

def planes(y):
    n, m = y.shape
    v = y.astype(np.float32).astype(ml_dtypes.bfloat16).astype(np.float64).reshape(n // 32, 32, m)
    top = np.abs(v).max(1)
    byte = np.clip(np.where(top > 0, np.frexp(top)[1] - 1 + 127 - 7, 1), 1, 254)
    codes = (v * np.exp2(127.0 - byte)[:, None, :]).reshape(n, m).astype(np.float32).astype(ml_dtypes.float8_e4m3fn).view(np.uint8)
    words = codes.reshape(n // 512, 128, 4, m).transpose(0, 1, 3, 2)
    return np.ascontiguousarray(words), np.ascontiguousarray(byte.astype(np.uint8).reshape(n // 512, 16, m))


K, T, S, H, C = 512, 2048, 512, 512, 512


def setup_inputs():
    n = np.random.standard_normal
    s = mx_kscale(K)[:, None]
    packed_xT = pack_weight(n((K, T)) * s)
    packed_w1 = pack_weight(n((K, H)) / np.sqrt(K) / s)
    return {
        "x_words": packed_xT[0],
        "x_scales": packed_xT[1],
        "w1_words": packed_w1[0],
        "w1_scales": packed_w1[1],
        "gs": (np.random.uniform(0.5, 1.5, (K, 1)) / s).astype(np.float32),
        "offs": striped8(np.random.randint(0, T, (8, S))),
        "n1": striped8(np.stack([np.random.permutation(S) for _ in range(8)])),
        "n2": striped8(np.stack([np.random.permutation(S) for _ in range(8)])),
        "cand": striped8(np.random.randint(0, T, (8, C))),
        "n3": striped8(np.stack([np.random.permutation(S) for _ in range(8)])),
        "n4": striped8(np.stack([np.random.permutation(S) for _ in range(8)])),
    }


def reference(x_words, x_scales, w1_words, w1_scales, gs, offs, n1, n2, cand, n3, n4):
    x_cand = unpack_weight(x_words, x_scales)[np.arange(K)[:, None], runs(cand, K)]
    xq = unpack_weight(x_words, x_scales)[np.arange(K)[:, None], runs(offs, K)]
    y = unpack_weight(w1_words, w1_scales).T @ xq
    ex = np.exp(0.5 * y)
    z = f64(gs) * ((2.0 * ex) / (ex + ex[np.arange(H)[:, None], runs(n1, H)] + ex[np.arange(H)[:, None], runs(n2, H)]))
    s = 0.0625 * ((x_cand.T @ mxq(z, 0, "e4m3")))
    out_0 = s + (sigmoid(s[np.arange(C)[:, None], runs(n3, C)])) * (s[np.arange(C)[:, None], runs(n4, C)] - s)
    return (out_0,) + planes(out_0)

@@ -1,0 +1,192 @@
+from contextlib import ExitStack
+
+import concourse.mybir as mybir
+
+F32 = mybir.dt.float32
+BF16 = mybir.dt.bfloat16
+I32 = mybir.dt.int32
+U32 = mybir.dt.uint32
+U16 = mybir.dt.uint16
+U8 = mybir.dt.uint8
+FP8X4 = mybir.dt.float8_e4m3fn_x4
+ACT = mybir.ActivationFunctionType
+ALU = mybir.AluOpType
+
+P, T, S = 128, 2048, 512
+FLOPS = 2 * 2 * 512 * 512 * 512
+SHARE_CHUNKS = [(0, 256), (256, 384), (384, 512)]
+MIX_CHUNKS = [(0, 128), (128, 384), (384, 512)]
+
+
+def tile_picked_hcandsharetrack_none_po_kernel(tc, x_words, x_scales, w1_words, w1_scales, gs, offs, n1, n2, cand, n3, n4, out_0, out_1, out_2):
+    nc = tc.nc
+    with ExitStack() as ctx:
+        keep = ctx.enter_context(tc.tile_pool(name="keep", bufs=1))
+        psum = ctx.enter_context(tc.psum_pool(name="psum", bufs=1))
+
+        def new(name, shape, dtype, tag=None):
+            return keep.tile(shape, dtype, name=name, tag=tag or name, align_bytes=64)
+
+        lists = {}
+        for name in ("offs", "cand", "n1", "n2", "n3", "n4"):
+            lists[name] = keep.tile([P, S // 16], U16, name="list_" + name)
+
+        def entries(name, a, b):
+            return lists[name][:, a // 16 : b // 16]
+
+        xw = new("xw", [P, T], I32)
+        xs = new("xs", [P, T], U8)
+        ww = new("ww", [P, S], I32)
+        ws = new("ws", [P, S], U8)
+        gain = new("gain", [P, 4], F32)
+        first_planes = new("first_planes", [P, 2 * S], U8)
+        c_plane = new("c_plane", [P, S], U8)
+
+        nc.scalar.dma_start(xw[:], x_words[0].rearrange("p n t -> p (n t)").bitcast(I32))
+        nc.sync.dma_start(lists["offs"][:], offs)
+        nc.sync.dma_start(xs[:].bitcast(I32), x_scales[0].bitcast(I32).unsqueeze(1).to_broadcast([16, 8, T // 4]))
+        nc.sync.dma_start(ws[:].bitcast(I32), w1_scales[0].bitcast(I32).unsqueeze(1).to_broadcast([16, 8, S // 4]))
+        nc.sync.dma_start(lists["cand"][:], cand)
+        nc.sync.dma_start(lists["n1"][:], n1)
+        nc.sync.dma_start(lists["n2"][:], n2)
+        nc.sync.dma_start(ww[:], w1_words[0].rearrange("p n t -> p (n t)").bitcast(I32))
+        nc.sync.dma_start(lists["n3"][:], n3)
+        nc.sync.dma_start(lists["n4"][:], n4)
+        nc.sync.dma_start(gain[:], gs.rearrange("(p t) o -> p (t o)", t=4))
+        nc.gpsimd.memset(first_planes[:].bitcast(I32), 0)
+        nc.gpsimd.memset(c_plane[:].bitcast(I32), 0)
+
+        def place_rows(plane, src, engine):
+            for i in range(4):
+                engine.dma_start(plane[i:P:32, :].bitcast(I32), src[8 * i : P : 32, :].bitcast(I32))
+
+        def deal(dst, src):
+            nc.vector.tensor_copy(dst.rearrange("p (t m) -> p m t", t=4), src.rearrange("p (m t) -> p m t", t=4))
+
+        q_bytes = new("q_bytes", [P, S], U8)
+        both = new("both", [P, 2 * S], U8)
+        nc.vector.tensor_copy(q_bytes[:], xs[:].indirect(lists["offs"][:]))
+        deal(both[:, S : 2 * S], ws[:])
+        nc.vector.tensor_copy(both[:, 0:S].bitcast(I32), q_bytes[:].bitcast(I32))
+        place_rows(first_planes, both, nc.scalar)
+        q_plane = first_planes[:, 0:S]
+        w_plane = first_planes[:, S : 2 * S]
+        q_words = new("q_words", [P, S], U32)
+        nc.vector.tensor_copy(q_words[:], xw[:].bitcast(U32).indirect(lists["offs"][:]))
+        wd = new("wd", [P, S], U32)
+        deal(wd[:], ww[:].bitcast(U32))
+
+        head = SHARE_CHUNKS[0][1]
+        ex = []
+        ex_head = new("ex_head", [P, 4, head], F32)
+        ex_rest = new("ex_rest", [P, 4, S - head], F32)
+        for t in range(4):
+            y = psum.tile([P, S], F32, name="y%d" % t)
+            cols = slice(t * P, (t + 1) * P)
+            nc.tensor.matmul_mx(out=y[:], lhsT=wd[:, cols].bitcast(FP8X4), lhsT_scale=w_plane[:, cols], rhs=q_words[:].bitcast(FP8X4), rhs_scale=q_plane, start=True, stop=True)
+            ex.append(new("ex%d" % t, [P, S], F32))
+            nc.scalar.activation(ex[t][:], y[:], ACT.Exp, scale=0.5)
+            nc.scalar.activation(ex_head[:, t, :], y[:, 0:head], ACT.Exp, scale=0.5)
+            nc.sync.dma_start(ex_rest[:, t, :], ex[t][:, head:S])
+
+        c_bytes = new("c_bytes", [P, S], U8)
+        nc.vector.tensor_copy(c_bytes[:], xs[:].indirect(lists["cand"][:]))
+        c_bytes_d = new("c_bytes_d", [P, S], U8)
+        deal(c_bytes_d[:], c_bytes[:])
+        c_words = new("c_words", [P, S], U32)
+        nc.vector.tensor_copy(c_words[:], xw[:].bitcast(U32).indirect(lists["cand"][:]))
+        cd = new("cd", [P, S], U32)
+        deal(cd[:], c_words[:])
+        place_rows(c_plane, c_bytes_d, nc.sync)
+
+        sbank = [psum.tile([P, S], F32, name="s%d" % t) for t in range(4)]
+        sw = [new("sw%d" % t, [P, S], F32) for t in range(4)]
+        z_words = new("z_words", [P, S], U32)
+        z_plane = new("z_plane", [P, S], U8)
+
+        def denominators(c, part_tag=None):
+            a, b = SHARE_CHUNKS[c]
+            part = new("part%d" % c, [P, 4, b - a], F32, part_tag)
+            den = new("den%d" % c, [P, 4, b - a], F32)
+            for t in range(5):
+                if t < 4:
+                    own = ex_head[:, t, :] if c == 0 else ex_rest[:, t, a - head : b - head]
+                    nc.vector.tensor_tensor(part[:, t, :], ex[t][:].indirect(entries("n1", a, b)), own, ALU.add)
+                if t > 0:
+                    nc.vector.tensor_tensor(den[:, t - 1, :], ex[t - 1][:].indirect(entries("n2", a, b)), part[:, t - 1, :], ALU.add)
+            return den
+
+        def numerators(name, a, b, tag=None):
+            num = new(name, [P, 4, b - a], F32, tag)
+            for t in range(4):
+                nc.scalar.activation(num[:, t, :], ex[t][:, a:b], ACT.Copy, scale=gain[:, t : t + 1])
+            return num
+
+        def inverse(c, den):
+            root = new("root%d" % c, den.shape, F32)
+            inv = new("inv%d" % c, den.shape, F32)
+            nc.scalar.activation(root[:], den[:], ACT.Abs_reciprocal_sqrt, scale=0.5)
+            nc.scalar.activation(inv[:], root[:], ACT.Square)
+            return inv
+
+        def scores(c, num, inv, zb_tag=None):
+            a, b = SHARE_CHUNKS[c]
+            zb = new("zb%d" % c, [P, (b - a) * 4], BF16, zb_tag)
+            nc.vector.tensor_tensor(zb[:].rearrange("p (c i t) -> p c t i", i=4, t=4), num.rearrange("p t (c i) -> p c t i", i=4), inv[:].rearrange("p t (c i) -> p c t i", i=4), ALU.mult)
+            nc.vector.quantize_mx(out=z_words[:, a:b].bitcast(FP8X4), scales=z_plane[:, a:b], in_=zb[:])
+            for t in range(4):
+                cols = slice(t * P, (t + 1) * P)
+                nc.tensor.matmul_mx(out=sbank[t][:, a:b], lhsT=cd[:, cols].bitcast(FP8X4), lhsT_scale=c_plane[:, cols], rhs=z_words[:, a:b].bitcast(FP8X4), rhs_scale=z_plane[:, a:b], start=True, stop=True)
+
+        num_head = numerators("num_head", 0, head)
+        den0 = denominators(0)
+        inv0 = inverse(0, den0)
+        den1 = denominators(1)
+        inv1 = inverse(1, den1)
+        num_rest = numerators("num_rest", head, S, "root0")
+        scores(0, num_head[:], inv0)
+        for t in range(4):
+            nc.scalar.activation(sw[t][:, 0:head], sbank[t][:, 0:head], ACT.Copy, scale=0.0625)
+        den2 = denominators(2, "inv0")
+        inv2 = inverse(2, den2)
+        scores(1, num_rest[:, :, 0:128], inv1, "inv0")
+        scores(2, num_rest[:, :, 128:256], inv2)
+        for t in range(4):
+            nc.vector.tensor_scalar(sw[t][:, head:S], sbank[t][:, head:S], 0.0625, None, ALU.mult)
+
+        o_words = new("o_words", [P, S], U32)
+        o_plane = new("o_plane", [P, S], U8)
+        out_rows = out_0.rearrange("(p t) j -> p t j", t=4)
+        out_words = out_1[0].rearrange("p n t -> p (n t)").bitcast(I32)
+
+        def mix(c):
+            a, b = MIX_CHUNKS[c]
+            gate = new("gate%d" % c, [P, 4, b - a], F32)
+            far = new("far%d" % c, [P, 4, b - a], F32)
+            near = new("near%d" % c, [P, 4, b - a], F32)
+            res = new("res%d" % c, [P, 4, b - a], F32)
+            for t in range(4):
+                nc.scalar.activation(gate[:, t, :], sw[t][:].indirect(entries("n3", a, b)), ACT.Sigmoid)
+                nc.vector.tensor_tensor(far[:, t, :], sw[t][:].indirect(entries("n4", a, b)), gate[:, t, :], ALU.mult)
+                nc.vector.scalar_tensor_tensor(near[:, t, :], gate[:, t, :], 1.0, sw[t][:, a:b], ALU.subtract, ALU.mult)
+            nc.vector.tensor_tensor(res[:], far[:], near[:], ALU.subtract)
+            nc.sync.dma_start(out_rows[:, :, a:b], res[:])
+            return res
+
+        def hand_on(c, res, copy, tag=None):
+            a, b = MIX_CHUNKS[c]
+            ob = new("ob%d" % c, [P, (b - a) * 4], BF16, tag)
+            copy(ob[:].rearrange("p (c i t) -> p c t i", i=4, t=4), res[:].rearrange("p t (c i) -> p c t i", i=4))
+            nc.vector.quantize_mx(out=o_words[:, a:b].bitcast(FP8X4), scales=o_plane[:, a:b], in_=ob[:])
+            nc.sync.dma_start(out_words[:, a:b], o_words[:, a:b].bitcast(I32))
+
+        res0 = mix(0)
+        res1 = mix(1)
+        res2 = mix(2)
+        hand_on(0, res0, nc.scalar.copy, "far1")
+        hand_on(1, res1, nc.scalar.copy)
+        hand_on(2, res2, nc.vector.tensor_copy)
+        out_scale_rows = out_2[0].bitcast(I32)
+        for i in range(4):
+            eng = nc.sync if i % 2 == 0 else nc.scalar
+            eng.dma_start(out_scale_rows[i:16:4, :], o_plane[i:P:32, :].bitcast(I32))

@@ -13,9 +13,8 @@ ACT = mybir.ActivationFunctionType
 ALU = mybir.AluOpType
 
 P, T, S = 128, 2048, 512
+H, Q = S // 2, S // 4
 FLOPS = 2 * 2 * 512 * 512 * 512
-SHARE_CHUNKS = [(0, 256), (256, 384), (384, 512)]
-MIX_CHUNKS = [(0, 128), (128, 384), (384, 512)]
 
 
 def tile_picked_hcandsharetrack_none_po_kernel(tc, x_words, x_scales, w1_words, w1_scales, gs, offs, n1, n2, cand, n3, n4, out_0, out_1, out_2):
@@ -41,8 +40,8 @@ def tile_picked_hcandsharetrack_none_po_kernel(tc, x_words, x_scales, w1_words, 
         gain = new("gain", [P, 4], F32)
         first_planes = new("first_planes", [P, 2 * S], U8)
         c_plane = new("c_plane", [P, S], U8)
+        win = [new("win%d" % t, [P, 2 * S], F32) for t in range(4)]
 
-        nc.scalar.dma_start(xw[:], x_words[0].rearrange("p n t -> p (n t)").bitcast(I32))
         nc.sync.dma_start(lists["offs"][:], offs)
         nc.sync.dma_start(xs[:].bitcast(I32), x_scales[0].bitcast(I32).unsqueeze(1).to_broadcast([16, 8, T // 4]))
         nc.sync.dma_start(ws[:].bitcast(I32), w1_scales[0].bitcast(I32).unsqueeze(1).to_broadcast([16, 8, S // 4]))
@@ -50,11 +49,13 @@ def tile_picked_hcandsharetrack_none_po_kernel(tc, x_words, x_scales, w1_words, 
         nc.sync.dma_start(lists["n1"][:], n1)
         nc.sync.dma_start(lists["n2"][:], n2)
         nc.sync.dma_start(ww[:], w1_words[0].rearrange("p n t -> p (n t)").bitcast(I32))
+        nc.sync.dma_start(xw[:], x_words[0].rearrange("p n t -> p (n t)").bitcast(I32))
         nc.sync.dma_start(lists["n3"][:], n3)
         nc.sync.dma_start(lists["n4"][:], n4)
         nc.sync.dma_start(gain[:], gs.rearrange("(p t) o -> p (t o)", t=4))
         nc.gpsimd.memset(first_planes[:].bitcast(I32), 0)
         nc.gpsimd.memset(c_plane[:].bitcast(I32), 0)
+        nc.gpsimd.memset(win[0][:, S : 2 * S], 0.0)
 
         def place_rows(plane, src, engine):
             for i in range(4):
@@ -75,23 +76,9 @@ def tile_picked_hcandsharetrack_none_po_kernel(tc, x_words, x_scales, w1_words, 
         nc.vector.tensor_copy(q_words[:], xw[:].bitcast(U32).indirect(lists["offs"][:]))
         wd = new("wd", [P, S], U32)
         deal(wd[:], ww[:].bitcast(U32))
-
-        head = SHARE_CHUNKS[0][1]
-        ex = []
-        ex_head = new("ex_head", [P, 4, head], F32)
-        ex_rest = new("ex_rest", [P, 4, S - head], F32)
-        for t in range(4):
-            y = psum.tile([P, S], F32, name="y%d" % t)
-            cols = slice(t * P, (t + 1) * P)
-            nc.tensor.matmul_mx(out=y[:], lhsT=wd[:, cols].bitcast(FP8X4), lhsT_scale=w_plane[:, cols], rhs=q_words[:].bitcast(FP8X4), rhs_scale=q_plane, start=True, stop=True)
-            ex.append(new("ex%d" % t, [P, S], F32))
-            nc.scalar.activation(ex[t][:], y[:], ACT.Exp, scale=0.5)
-            nc.scalar.activation(ex_head[:, t, :], y[:, 0:head], ACT.Exp, scale=0.5)
-            nc.sync.dma_start(ex_rest[:, t, :], ex[t][:, head:S])
-
         c_bytes = new("c_bytes", [P, S], U8)
         nc.vector.tensor_copy(c_bytes[:], xs[:].indirect(lists["cand"][:]))
-        c_bytes_d = new("c_bytes_d", [P, S], U8)
+        c_bytes_d = new("c_bytes_d", [P, S], U8, "both")
         deal(c_bytes_d[:], c_bytes[:])
         c_words = new("c_words", [P, S], U32)
         nc.vector.tensor_copy(c_words[:], xw[:].bitcast(U32).indirect(lists["cand"][:]))
@@ -99,93 +86,88 @@ def tile_picked_hcandsharetrack_none_po_kernel(tc, x_words, x_scales, w1_words, 
         deal(cd[:], c_words[:])
         place_rows(c_plane, c_bytes_d, nc.sync)
 
-        sbank = [psum.tile([P, S], F32, name="s%d" % t) for t in range(4)]
-        sw = [new("sw%d" % t, [P, S], F32) for t in range(4)]
+        own_last = new("own", [P, S], F32)
+        own = [win[1][:, S : 2 * S], win[2][:, S : 2 * S], win[3][:, S : 2 * S], own_last[:]]
+        part = new("part", [P, 4, S], F32)
+        for t in range(4):
+            y = psum.tile([P, S], F32, name="y%d" % t)
+            cols = slice(t * P, (t + 1) * P)
+            nc.tensor.matmul_mx(out=y[:], lhsT=wd[:, cols].bitcast(FP8X4), lhsT_scale=w_plane[:, cols], rhs=q_words[:].bitcast(FP8X4), rhs_scale=q_plane, start=True, stop=True)
+            nc.scalar.activation(win[t][:, 0:S], y[:], ACT.Exp, scale=0.5)
+            nc.scalar.activation(own[t], y[:], ACT.Exp, scale=0.5)
+            nc.vector.tensor_tensor(part[:, t, :], win[t][:].indirect(lists["n1"][:]), own[t], ALU.add)
+        num = new("num", [P, 4, S], F32, "wd")
+        for t in range(4):
+            nc.scalar.activation(num[:, t, :], own[t], ACT.Copy, scale=gain[:, t : t + 1])
+        den = [new("den%d" % h, [P, 4, H], F32, "own" if h == 1 else None) for h in range(2)]
+        for h in range(2):
+            for t in range(4):
+                nc.vector.tensor_tensor(den[h][:, t, :], win[t][:].indirect(entries("n2", h * H, (h + 1) * H)), part[:, t, h * H : (h + 1) * H], ALU.add)
+
+        sbank = [[psum.tile([P, H], F32, name="s%d_%d" % (h, t), tag=("s%d", "y%d")[h] % t) for t in range(4)] for h in range(2)]
         z_words = new("z_words", [P, S], U32)
         z_plane = new("z_plane", [P, S], U8)
-
-        def denominators(c, part_tag=None):
-            a, b = SHARE_CHUNKS[c]
-            part = new("part%d" % c, [P, 4, b - a], F32, part_tag)
-            den = new("den%d" % c, [P, 4, b - a], F32)
-            for t in range(5):
-                if t < 4:
-                    own = ex_head[:, t, :] if c == 0 else ex_rest[:, t, a - head : b - head]
-                    nc.vector.tensor_tensor(part[:, t, :], ex[t][:].indirect(entries("n1", a, b)), own, ALU.add)
-                if t > 0:
-                    nc.vector.tensor_tensor(den[:, t - 1, :], ex[t - 1][:].indirect(entries("n2", a, b)), part[:, t - 1, :], ALU.add)
-            return den
-
-        def numerators(name, a, b, tag=None):
-            num = new(name, [P, 4, b - a], F32, tag)
-            for t in range(4):
-                nc.scalar.activation(num[:, t, :], ex[t][:, a:b], ACT.Copy, scale=gain[:, t : t + 1])
-            return num
-
-        def inverse(c, den):
-            root = new("root%d" % c, den.shape, F32)
-            inv = new("inv%d" % c, den.shape, F32)
-            nc.scalar.activation(root[:], den[:], ACT.Abs_reciprocal_sqrt, scale=0.5)
-            nc.scalar.activation(inv[:], root[:], ACT.Square)
-            return inv
-
-        def scores(c, num, inv, zb_tag=None):
-            a, b = SHARE_CHUNKS[c]
-            zb = new("zb%d" % c, [P, (b - a) * 4], BF16, zb_tag)
-            nc.vector.tensor_tensor(zb[:].rearrange("p (c i t) -> p c t i", i=4, t=4), num.rearrange("p t (c i) -> p c t i", i=4), inv[:].rearrange("p t (c i) -> p c t i", i=4), ALU.mult)
+        pieces = [(0, H), (H, H + Q), (H + Q, S)]
+        inv = new("inv", [P, 4, S], F32)
+        for h in range(2):
+            root = new("root%d" % h, [P, 4, H], F32, "root")
+            nc.scalar.activation(root[:], den[h][:], ACT.Abs_reciprocal_sqrt, scale=0.5)
+            for a, b in pieces:
+                if a // H == h:
+                    nc.scalar.activation(inv[:, :, a:b], root[:, :, a - h * H : b - h * H], ACT.Square)
+        for c, (a, b) in enumerate(pieces):
+            zb = new("zb%d" % c, [P, (b - a) * 4], BF16, "part" if c == 0 else None)
+            nc.vector.tensor_tensor(zb[:].rearrange("p (c i t) -> p c t i", i=4, t=4), num[:, :, a:b].rearrange("p t (c i) -> p c t i", i=4), inv[:, :, a:b].rearrange("p t (c i) -> p c t i", i=4), ALU.mult)
             nc.vector.quantize_mx(out=z_words[:, a:b].bitcast(FP8X4), scales=z_plane[:, a:b], in_=zb[:])
             for t in range(4):
                 cols = slice(t * P, (t + 1) * P)
-                nc.tensor.matmul_mx(out=sbank[t][:, a:b], lhsT=cd[:, cols].bitcast(FP8X4), lhsT_scale=c_plane[:, cols], rhs=z_words[:, a:b].bitcast(FP8X4), rhs_scale=z_plane[:, a:b], start=True, stop=True)
-
-        num_head = numerators("num_head", 0, head)
-        den0 = denominators(0)
-        inv0 = inverse(0, den0)
-        den1 = denominators(1)
-        inv1 = inverse(1, den1)
-        num_rest = numerators("num_rest", head, S, "root0")
-        scores(0, num_head[:], inv0)
-        for t in range(4):
-            nc.scalar.activation(sw[t][:, 0:head], sbank[t][:, 0:head], ACT.Copy, scale=0.0625)
-        den2 = denominators(2, "inv0")
-        inv2 = inverse(2, den2)
-        scores(1, num_rest[:, :, 0:128], inv1, "inv0")
-        scores(2, num_rest[:, :, 128:256], inv2)
-        for t in range(4):
-            nc.vector.tensor_scalar(sw[t][:, head:S], sbank[t][:, head:S], 0.0625, None, ALU.mult)
+                nc.tensor.matmul_mx(out=sbank[a // H][t][:, a % H : a % H + b - a], lhsT=cd[:, cols].bitcast(FP8X4), lhsT_scale=c_plane[:, cols], rhs=z_words[:, a:b].bitcast(FP8X4), rhs_scale=z_plane[:, a:b], start=True, stop=True)
 
         o_words = new("o_words", [P, S], U32)
         o_plane = new("o_plane", [P, S], U8)
         out_rows = out_0.rearrange("(p t) j -> p t j", t=4)
         out_words = out_1[0].rearrange("p n t -> p (n t)").bitcast(I32)
+        gate = new("gate", [P, 4, S], F32)
+        far = new("far", [P, 4, S], F32)
+        near = new("near", [P, 4, S], F32)
+        res = new("res", [P, 4, S], F32)
 
-        def mix(c):
-            a, b = MIX_CHUNKS[c]
-            gate = new("gate%d" % c, [P, 4, b - a], F32)
-            far = new("far%d" % c, [P, 4, b - a], F32)
-            near = new("near%d" % c, [P, 4, b - a], F32)
-            res = new("res%d" % c, [P, 4, b - a], F32)
-            for t in range(4):
-                nc.scalar.activation(gate[:, t, :], sw[t][:].indirect(entries("n3", a, b)), ACT.Sigmoid)
-                nc.vector.tensor_tensor(far[:, t, :], sw[t][:].indirect(entries("n4", a, b)), gate[:, t, :], ALU.mult)
-                nc.vector.scalar_tensor_tensor(near[:, t, :], gate[:, t, :], 1.0, sw[t][:, a:b], ALU.subtract, ALU.mult)
-            nc.vector.tensor_tensor(res[:], far[:], near[:], ALU.subtract)
-            nc.sync.dma_start(out_rows[:, :, a:b], res[:])
-            return res
+        def mix(t, a, b):
+            nc.scalar.activation(gate[:, t, a:b], win[t][:].indirect(entries("n3", a, b)), ACT.Sigmoid)
+            nc.vector.tensor_tensor(far[:, t, a:b], win[t][:].indirect(entries("n4", a, b)), gate[:, t, a:b], ALU.mult)
+            nc.vector.scalar_tensor_tensor(near[:, t, a:b], gate[:, t, a:b], 1.0, win[t][:, a:b], ALU.subtract, ALU.mult)
 
-        def hand_on(c, res, copy, tag=None):
-            a, b = MIX_CHUNKS[c]
-            ob = new("ob%d" % c, [P, (b - a) * 4], BF16, tag)
-            copy(ob[:].rearrange("p (c i t) -> p c t i", i=4, t=4), res[:].rearrange("p t (c i) -> p c t i", i=4))
+        def finish(t, a, b):
+            nc.vector.tensor_tensor(res[:, t, a:b], far[:, t, a:b], near[:, t, a:b], ALU.subtract)
+            nc.sync.dma_start(out_rows[:, t, a:b], res[:, t, a:b])
+
+        def hand_on(a, b, copy):
+            ob = new("ob%d" % a, [P, (b - a) * 4], BF16)
+            copy(ob[:].rearrange("p (c i t) -> p c t i", i=4, t=4), res[:, :, a:b].rearrange("p t (c i) -> p c t i", i=4))
             nc.vector.quantize_mx(out=o_words[:, a:b].bitcast(FP8X4), scales=o_plane[:, a:b], in_=ob[:])
             nc.sync.dma_start(out_words[:, a:b], o_words[:, a:b].bitcast(I32))
 
-        res0 = mix(0)
-        res1 = mix(1)
-        res2 = mix(2)
-        hand_on(0, res0, nc.scalar.copy, "far1")
-        hand_on(1, res1, nc.scalar.copy)
-        hand_on(2, res2, nc.vector.tensor_copy)
+        for t in range(2):
+            nc.scalar.activation(win[t][:, 0:H], sbank[0][t][:], ACT.Copy, scale=0.0625)
+        for t in range(2, 4):
+            nc.vector.tensor_scalar(win[t][:, 0:H], sbank[0][t][:], 0.0625, None, ALU.mult)
+        for t in range(4):
+            nc.vector.tensor_scalar(win[t][:, H:S], sbank[1][t][:], 0.0625, None, ALU.mult)
+        for t in range(4):
+            if t == 0:
+                mix(t, 0, H)
+                mix(t, H, S)
+                finish(t, 0, S)
+            elif t == 3:
+                mix(t, 0, H)
+                finish(t, 0, H)
+                mix(t, H, S)
+                finish(t, H, S)
+            else:
+                mix(t, 0, S)
+                finish(t, 0, S)
+        hand_on(0, H, nc.scalar.copy)
+        hand_on(H, S, nc.vector.tensor_copy)
         out_scale_rows = out_2[0].bitcast(I32)
         for i in range(4):
             eng = nc.sync if i % 2 == 0 else nc.scalar

@@ -42,9 +42,9 @@ def tile_picked_hcandsharetrack_none_po_kernel(tc, x_words, x_scales, w1_words, 
         c_plane = new("c_plane", [P, S], U8)
         win = [new("win%d" % t, [P, 2 * S], F32) for t in range(4)]
 
+        nc.sync.dma_start(ws[:].bitcast(I32), w1_scales[0].bitcast(I32).unsqueeze(1).to_broadcast([16, 8, S // 4]))
         nc.sync.dma_start(lists["offs"][:], offs)
         nc.sync.dma_start(xs[:].bitcast(I32), x_scales[0].bitcast(I32).unsqueeze(1).to_broadcast([16, 8, T // 4]))
-        nc.sync.dma_start(ws[:].bitcast(I32), w1_scales[0].bitcast(I32).unsqueeze(1).to_broadcast([16, 8, S // 4]))
         nc.sync.dma_start(lists["cand"][:], cand)
         nc.sync.dma_start(lists["n1"][:], n1)
         nc.sync.dma_start(lists["n2"][:], n2)
@@ -57,19 +57,19 @@ def tile_picked_hcandsharetrack_none_po_kernel(tc, x_words, x_scales, w1_words, 
         nc.gpsimd.memset(c_plane[:].bitcast(I32), 0)
         nc.gpsimd.memset(win[0][:, S : 2 * S], 0.0)
 
-        def place_rows(plane, src, engine):
+        def place_rows(plane, src, engines):
             for i in range(4):
-                engine.dma_start(plane[i:P:32, :].bitcast(I32), src[8 * i : P : 32, :].bitcast(I32))
+                engines[i % 2].dma_start(plane[i:P:32, :].bitcast(I32), src[8 * i : P : 32, :].bitcast(I32))
 
         def deal(dst, src):
             nc.vector.tensor_copy(dst.rearrange("p (t m) -> p m t", t=4), src.rearrange("p (m t) -> p m t", t=4))
 
         q_bytes = new("q_bytes", [P, S], U8)
         both = new("both", [P, 2 * S], U8)
-        nc.vector.tensor_copy(q_bytes[:], xs[:].indirect(lists["offs"][:]))
         deal(both[:, S : 2 * S], ws[:])
+        nc.vector.tensor_copy(q_bytes[:], xs[:].indirect(lists["offs"][:]))
         nc.vector.tensor_copy(both[:, 0:S].bitcast(I32), q_bytes[:].bitcast(I32))
-        place_rows(first_planes, both, nc.scalar)
+        place_rows(first_planes, both, (nc.sync, nc.scalar))
         q_plane = first_planes[:, 0:S]
         w_plane = first_planes[:, S : 2 * S]
         q_words = new("q_words", [P, S], U32)
@@ -84,7 +84,7 @@ def tile_picked_hcandsharetrack_none_po_kernel(tc, x_words, x_scales, w1_words, 
         nc.vector.tensor_copy(c_words[:], xw[:].bitcast(U32).indirect(lists["cand"][:]))
         cd = new("cd", [P, S], U32)
         deal(cd[:], c_words[:])
-        place_rows(c_plane, c_bytes_d, nc.sync)
+        place_rows(c_plane, c_bytes_d, (nc.sync, nc.sync))
 
         own_last = new("own", [P, S], F32)
         own = [win[1][:, S : 2 * S], win[2][:, S : 2 * S], win[3][:, S : 2 * S], own_last[:]]
@@ -132,14 +132,20 @@ def tile_picked_hcandsharetrack_none_po_kernel(tc, x_words, x_scales, w1_words, 
         near = new("near", [P, 4, S], F32)
         res = new("res", [P, 4, S], F32)
 
-        def mix(t, a, b):
-            nc.scalar.activation(gate[:, t, a:b], win[t][:].indirect(entries("n3", a, b)), ACT.Sigmoid)
-            nc.vector.tensor_tensor(far[:, t, a:b], win[t][:].indirect(entries("n4", a, b)), gate[:, t, a:b], ALU.mult)
-            nc.vector.scalar_tensor_tensor(near[:, t, a:b], gate[:, t, a:b], 1.0, win[t][:, a:b], ALU.subtract, ALU.mult)
+        sw = [win[0], win[1], new("sw2", [P, S], F32, "zb2"), new("sw3", [P, S], F32, "inv")]
 
-        def finish(t, a, b):
-            nc.vector.tensor_tensor(res[:, t, a:b], far[:, t, a:b], near[:, t, a:b], ALU.subtract)
-            nc.sync.dma_start(out_rows[:, t, a:b], res[:, t, a:b])
+        def gates(t, a, b):
+            nc.scalar.activation(gate[:, t, a:b], sw[t][:].indirect(entries("n3", a, b)), ACT.Sigmoid)
+
+        def far_term(t, a, b):
+            nc.vector.tensor_tensor(far[:, t, a:b], sw[t][:].indirect(entries("n4", a, b)), gate[:, t, a:b], ALU.mult)
+
+        def near_term(t, a, b):
+            nc.vector.scalar_tensor_tensor(near[:, t, a:b], gate[:, t, a:b], 1.0, sw[t][:, a:b], ALU.subtract, ALU.mult)
+
+        def finish(tiles, a, b):
+            nc.vector.tensor_tensor(res[:, tiles, a:b], far[:, tiles, a:b], near[:, tiles, a:b], ALU.subtract)
+            nc.sync.dma_start(out_rows[:, tiles, a:b], res[:, tiles, a:b])
 
         def hand_on(a, b, copy):
             ob = new("ob%d" % a, [P, (b - a) * 4], BF16)
@@ -148,26 +154,28 @@ def tile_picked_hcandsharetrack_none_po_kernel(tc, x_words, x_scales, w1_words, 
             nc.sync.dma_start(out_words[:, a:b], o_words[:, a:b].bitcast(I32))
 
         for t in range(2):
-            nc.scalar.activation(win[t][:, 0:H], sbank[0][t][:], ACT.Copy, scale=0.0625)
+            nc.scalar.activation(sw[t][:, 0:H], sbank[0][t][:], ACT.Copy, scale=0.0625)
         for t in range(2, 4):
-            nc.vector.tensor_scalar(win[t][:, 0:H], sbank[0][t][:], 0.0625, None, ALU.mult)
+            nc.vector.tensor_scalar(sw[t][:, 0:H], sbank[0][t][:], 0.0625, None, ALU.mult)
         for t in range(4):
-            nc.vector.tensor_scalar(win[t][:, H:S], sbank[1][t][:], 0.0625, None, ALU.mult)
-        for t in range(4):
-            if t == 0:
-                mix(t, 0, H)
-                mix(t, H, S)
-                finish(t, 0, S)
-            elif t == 3:
-                mix(t, 0, H)
-                finish(t, 0, H)
-                mix(t, H, S)
-                finish(t, H, S)
-            else:
-                mix(t, 0, S)
-                finish(t, 0, S)
-        hand_on(0, H, nc.scalar.copy)
-        hand_on(H, S, nc.vector.tensor_copy)
+            nc.vector.tensor_scalar(sw[t][:, H:S], sbank[1][t][:], 0.0625, None, ALU.mult)
+        for a, b in [(0, H), (H, S)]:
+            gates(0, a, b)
+            far_term(0, a, b)
+        near_term(0, 0, S)
+        finish(slice(0, 1), 0, S)
+        gates(1, 0, S)
+        far_term(1, 0, S)
+        near_term(1, 0, S)
+        finish(slice(1, 2), 0, S)
+        for a, b in pieces:
+            for t in (2, 3):
+                gates(t, a, b)
+                far_term(t, a, b)
+                near_term(t, a, b)
+            finish(slice(2, 4), a, b)
+        for a, b in pieces:
+            hand_on(a, b, nc.vector.tensor_copy if b == S else nc.scalar.copy)
         out_scale_rows = out_2[0].bitcast(I32)
         for i in range(4):
             eng = nc.sync if i % 2 == 0 else nc.scalar

from contextlib import ExitStack

import concourse.mybir as mybir

F32 = mybir.dt.float32
BF16 = mybir.dt.bfloat16
I32 = mybir.dt.int32
U32 = mybir.dt.uint32
U16 = mybir.dt.uint16
U8 = mybir.dt.uint8
FP8X4 = mybir.dt.float8_e4m3fn_x4
ACT = mybir.ActivationFunctionType
ALU = mybir.AluOpType

P, T, S = 128, 2048, 512
H, Q = S // 2, S // 4
FLOPS = 2 * 2 * 512 * 512 * 512


def tile_picked_hcandsharetrack_none_po_kernel(tc, x_words, x_scales, w1_words, w1_scales, gs, offs, n1, n2, cand, n3, n4, out_0, out_1, out_2):
    nc = tc.nc
    with ExitStack() as ctx:
        keep = ctx.enter_context(tc.tile_pool(name="keep", bufs=1))
        psum = ctx.enter_context(tc.psum_pool(name="psum", bufs=1))

        def new(name, shape, dtype, tag=None):
            return keep.tile(shape, dtype, name=name, tag=tag or name, align_bytes=64)

        lists = {}
        for name in ("offs", "cand", "n1", "n2", "n3", "n4"):
            lists[name] = keep.tile([P, S // 16], U16, name="list_" + name)

        def entries(name, a, b):
            return lists[name][:, a // 16 : b // 16]

        xw = new("xw", [P, T], I32)
        xs = new("xs", [P, T], U8)
        ww = new("ww", [P, S], I32)
        ws = new("ws", [P, S], U8)
        gain = new("gain", [P, 4], F32)
        first_planes = new("first_planes", [P, 2 * S], U8)
        c_plane = new("c_plane", [P, S], U8)
        win = [new("win%d" % t, [P, 2 * S], F32) for t in range(4)]

        nc.sync.dma_start(ws[:].bitcast(I32), w1_scales[0].bitcast(I32).unsqueeze(1).to_broadcast([16, 8, S // 4]))
        nc.sync.dma_start(lists["offs"][:], offs)
        nc.sync.dma_start(xs[:].bitcast(I32), x_scales[0].bitcast(I32).unsqueeze(1).to_broadcast([16, 8, T // 4]))
        nc.sync.dma_start(lists["cand"][:], cand)
        nc.sync.dma_start(lists["n1"][:], n1)
        nc.sync.dma_start(lists["n2"][:], n2)
        nc.sync.dma_start(ww[:], w1_words[0].rearrange("p n t -> p (n t)").bitcast(I32))
        nc.sync.dma_start(xw[:], x_words[0].rearrange("p n t -> p (n t)").bitcast(I32))
        nc.sync.dma_start(lists["n3"][:], n3)
        nc.sync.dma_start(lists["n4"][:], n4)
        nc.sync.dma_start(gain[:], gs.rearrange("(p t) o -> p (t o)", t=4))
        nc.gpsimd.memset(first_planes[:].bitcast(I32), 0)
        nc.gpsimd.memset(c_plane[:].bitcast(I32), 0)
        nc.gpsimd.memset(win[0][:, S : 2 * S], 0.0)

        def place_rows(plane, src, engines):
            for i in range(4):
                engines[i % 2].dma_start(plane[i:P:32, :].bitcast(I32), src[8 * i : P : 32, :].bitcast(I32))

        def deal(dst, src):
            nc.vector.tensor_copy(dst.rearrange("p (t m) -> p m t", t=4), src.rearrange("p (m t) -> p m t", t=4))

        q_bytes = new("q_bytes", [P, S], U8)
        both = new("both", [P, 2 * S], U8)
        deal(both[:, S : 2 * S], ws[:])
        nc.vector.tensor_copy(q_bytes[:], xs[:].indirect(lists["offs"][:]))
        nc.vector.tensor_copy(both[:, 0:S].bitcast(I32), q_bytes[:].bitcast(I32))
        place_rows(first_planes, both, (nc.sync, nc.scalar))
        q_plane = first_planes[:, 0:S]
        w_plane = first_planes[:, S : 2 * S]
        q_words = new("q_words", [P, S], U32)
        nc.vector.tensor_copy(q_words[:], xw[:].bitcast(U32).indirect(lists["offs"][:]))
        wd = new("wd", [P, S], U32)
        deal(wd[:], ww[:].bitcast(U32))
        c_bytes = new("c_bytes", [P, S], U8)
        nc.vector.tensor_copy(c_bytes[:], xs[:].indirect(lists["cand"][:]))
        c_bytes_d = new("c_bytes_d", [P, S], U8, "both")
        deal(c_bytes_d[:], c_bytes[:])
        c_words = new("c_words", [P, S], U32)
        nc.vector.tensor_copy(c_words[:], xw[:].bitcast(U32).indirect(lists["cand"][:]))
        cd = new("cd", [P, S], U32)
        deal(cd[:], c_words[:])
        place_rows(c_plane, c_bytes_d, (nc.sync, nc.sync))

        own_last = new("own", [P, S], F32)
        own = [win[1][:, S : 2 * S], win[2][:, S : 2 * S], win[3][:, S : 2 * S], own_last[:]]
        part = new("part", [P, 4, S], F32)
        for t in range(4):
            y = psum.tile([P, S], F32, name="y%d" % t)
            cols = slice(t * P, (t + 1) * P)
            nc.tensor.matmul_mx(out=y[:], lhsT=wd[:, cols].bitcast(FP8X4), lhsT_scale=w_plane[:, cols], rhs=q_words[:].bitcast(FP8X4), rhs_scale=q_plane, start=True, stop=True)
            nc.scalar.activation(win[t][:, 0:S], y[:], ACT.Exp, scale=0.5)
            nc.scalar.activation(own[t], y[:], ACT.Exp, scale=0.5)
            nc.vector.tensor_tensor(part[:, t, :], win[t][:].indirect(lists["n1"][:]), own[t], ALU.add)
        num = new("num", [P, 4, S], F32, "wd")
        for t in range(4):
            nc.scalar.activation(num[:, t, :], own[t], ACT.Copy, scale=gain[:, t : t + 1])
        den = [new("den%d" % h, [P, 4, H], F32, "own" if h == 1 else None) for h in range(2)]
        for h in range(2):
            for t in range(4):
                nc.vector.tensor_tensor(den[h][:, t, :], win[t][:].indirect(entries("n2", h * H, (h + 1) * H)), part[:, t, h * H : (h + 1) * H], ALU.add)

        sbank = [[psum.tile([P, H], F32, name="s%d_%d" % (h, t), tag=("s%d", "y%d")[h] % t) for t in range(4)] for h in range(2)]
        z_words = new("z_words", [P, S], U32)
        z_plane = new("z_plane", [P, S], U8)
        pieces = [(0, H), (H, H + Q), (H + Q, S)]
        inv = new("inv", [P, 4, S], F32)
        for h in range(2):
            root = new("root%d" % h, [P, 4, H], F32, "root")
            nc.scalar.activation(root[:], den[h][:], ACT.Abs_reciprocal_sqrt, scale=0.5)
            for a, b in pieces:
                if a // H == h:
                    nc.scalar.activation(inv[:, :, a:b], root[:, :, a - h * H : b - h * H], ACT.Square)
        for c, (a, b) in enumerate(pieces):
            zb = new("zb%d" % c, [P, (b - a) * 4], BF16, "part" if c == 0 else None)
            nc.vector.tensor_tensor(zb[:].rearrange("p (c i t) -> p c t i", i=4, t=4), num[:, :, a:b].rearrange("p t (c i) -> p c t i", i=4), inv[:, :, a:b].rearrange("p t (c i) -> p c t i", i=4), ALU.mult)
            nc.vector.quantize_mx(out=z_words[:, a:b].bitcast(FP8X4), scales=z_plane[:, a:b], in_=zb[:])
            for t in range(4):
                cols = slice(t * P, (t + 1) * P)
                nc.tensor.matmul_mx(out=sbank[a // H][t][:, a % H : a % H + b - a], lhsT=cd[:, cols].bitcast(FP8X4), lhsT_scale=c_plane[:, cols], rhs=z_words[:, a:b].bitcast(FP8X4), rhs_scale=z_plane[:, a:b], start=True, stop=True)

        o_words = new("o_words", [P, S], U32)
        o_plane = new("o_plane", [P, S], U8)
        out_rows = out_0.rearrange("(p t) j -> p t j", t=4)
        out_words = out_1[0].rearrange("p n t -> p (n t)").bitcast(I32)
        gate = new("gate", [P, 4, S], F32)
        far = new("far", [P, 4, S], F32)
        near = new("near", [P, 4, S], F32)
        res = new("res", [P, 4, S], F32)

        sw = [win[0], win[1], new("sw2", [P, S], F32, "zb2"), new("sw3", [P, S], F32, "inv")]

        def gates(t, a, b):
            nc.scalar.activation(gate[:, t, a:b], sw[t][:].indirect(entries("n3", a, b)), ACT.Sigmoid)

        def far_term(t, a, b):
            nc.vector.tensor_tensor(far[:, t, a:b], sw[t][:].indirect(entries("n4", a, b)), gate[:, t, a:b], ALU.mult)

        def near_term(t, a, b):
            nc.vector.scalar_tensor_tensor(near[:, t, a:b], gate[:, t, a:b], 1.0, sw[t][:, a:b], ALU.subtract, ALU.mult)

        def finish(tiles, a, b):
            nc.vector.tensor_tensor(res[:, tiles, a:b], far[:, tiles, a:b], near[:, tiles, a:b], ALU.subtract)
            nc.sync.dma_start(out_rows[:, tiles, a:b], res[:, tiles, a:b])

        def hand_on(a, b, copy):
            ob = new("ob%d" % a, [P, (b - a) * 4], BF16)
            copy(ob[:].rearrange("p (c i t) -> p c t i", i=4, t=4), res[:, :, a:b].rearrange("p t (c i) -> p c t i", i=4))
            nc.vector.quantize_mx(out=o_words[:, a:b].bitcast(FP8X4), scales=o_plane[:, a:b], in_=ob[:])
            nc.sync.dma_start(out_words[:, a:b], o_words[:, a:b].bitcast(I32))

        for t in range(2):
            nc.scalar.activation(sw[t][:, 0:H], sbank[0][t][:], ACT.Copy, scale=0.0625)
        for t in range(2, 4):
            nc.vector.tensor_scalar(sw[t][:, 0:H], sbank[0][t][:], 0.0625, None, ALU.mult)
        for t in range(4):
            nc.vector.tensor_scalar(sw[t][:, H:S], sbank[1][t][:], 0.0625, None, ALU.mult)
        for a, b in [(0, H), (H, S)]:
            gates(0, a, b)
            far_term(0, a, b)
        near_term(0, 0, S)
        finish(slice(0, 1), 0, S)
        gates(1, 0, S)
        far_term(1, 0, S)
        near_term(1, 0, S)
        finish(slice(1, 2), 0, S)
        for a, b in pieces:
            for t in (2, 3):
                gates(t, a, b)
                far_term(t, a, b)
                near_term(t, a, b)
            finish(slice(2, 4), a, b)
        for a, b in pieces:
            hand_on(a, b, nc.vector.tensor_copy if b == S else nc.scalar.copy)
        out_scale_rows = out_2[0].bitcast(I32)
        for i in range(4):
            eng = nc.sync if i % 2 == 0 else nc.scalar
            eng.dma_start(out_scale_rows[i:16:4, :], o_plane[i:P:32, :].bitcast(I32))
